import numpy as np
import ml_dtypes


def mxq(x, axis, fmt="e4m3"):
    dtype, down = {"e4m3": (ml_dtypes.float8_e4m3fn, 7), "e5m2": (ml_dtypes.float8_e5m2, 14)}[fmt]
    v = np.moveaxis(np.asarray(x, np.float32).astype(ml_dtypes.bfloat16).astype(np.float64), axis, -1)
    blocks = v.reshape(v.shape[:-1] + (-1, 32))
    amax = np.abs(blocks).max(-1, keepdims=True)
    byte = np.maximum(np.where(amax > 0, np.frexp(amax)[1] - 1 + 127, 0) - down, 1)
    scale = np.exp2(byte - 127.0)
    codes = (blocks / scale).astype(np.float32).astype(dtype).astype(np.float64)
    return np.moveaxis((codes * scale).reshape(v.shape), -1, axis)


WIDE = False


def mx_kscale(k):
    if not WIDE:
        return np.ones(k)
    levels = np.array([10, -10, 5, -5, 0])
    if k % 512:
        return np.exp2(np.random.permutation(np.resize(levels, k // 32))).repeat(32)
    a = np.empty((k // 512, 16))
    for p in range(k // 512):
        a[p, :8] = np.random.permutation(np.resize(levels, 8))
        for g in range(8):
            far = levels[np.abs(levels - a[p, g]) >= 10]
            a[p, g + 8] = far[np.random.randint(len(far))]
    return np.exp2(a.ravel()).repeat(32)


def f64(x):
    return np.asarray(x).astype(np.float64)


def striped(idx):
    return np.tile(idx.reshape(-1, 16).T, (8, 1)).astype(np.uint16)


def unstriped(offs):
    return offs[:16].T.reshape(-1).astype(np.int64)


def striped8(idx):
    return np.concatenate([x.reshape(-1, 16).T for x in idx]).astype(np.uint16)


def runs(offs, k):
    lists = np.stack([offs[16 * r : 16 * r + 16].T.reshape(-1) for r in range(8)]).astype(np.int64)
    return lists[np.arange(k) % 512 // 64]


def pack_weight(w):
    k, n = w.shape
    w = f64(np.asarray(w, np.float32).astype(ml_dtypes.bfloat16)).reshape(k // 32, 32, n)
    amax = np.abs(w).max(1)
    byte = np.clip(np.where(amax > 0, np.frexp(amax)[1] - 1 + 127 - 7, 1), 1, 254)
    scaled = (w * np.exp2(127.0 - byte)[:, None, :]).reshape(k, n).astype(np.float32)
    words = np.ascontiguousarray(scaled.reshape(k // 512, 128, 4, n).transpose(0, 1, 3, 2)).astype(ml_dtypes.float8_e4m3fn).view(np.uint8)
    return words, np.ascontiguousarray(byte.astype(np.uint8).reshape(k // 512, 16, n))


def unpack_weight(words, scales):
    g, p, n, _ = words.shape
    vals = np.ascontiguousarray(words).view(ml_dtypes.float8_e4m3fn).astype(np.float64) * np.repeat(np.exp2(scales.astype(np.float64) - 127.0), 8, axis=1)[..., None]
    return vals.transpose(0, 1, 3, 2).reshape(g * 512, n)


K, T, S, N, H, U = 512, 2048, 512, 512, 512, 1024


def setup_inputs():
    n = np.random.standard_normal
    s = mx_kscale(K)[:, None]
    u = mx_kscale(H)
    packed_xT = pack_weight(n((K, T)) * s)
    return {
        "x_words": packed_xT[0],
        "x_scales": packed_xT[1],
        "w1": (n((K, H)) / np.sqrt(K) / s).astype(np.float32),
        "gn": (np.random.uniform(0.5, 1.5, (H, 1)) * u[:, None]).astype(np.float32),
        "w2": (n((H, N)) / np.sqrt(H) / u[:, None]).astype(np.float32),
        "mem": n((N, U)).astype(np.float32),
        "offs": striped(np.random.permutation(T)[:S]),
        "rt": striped8(np.stack([np.random.permutation(S) for _ in range(8)])),
        "lf": striped8(np.stack([np.random.permutation(S) for _ in range(8)])),
        "up": striped8(np.stack([np.random.permutation(S) for _ in range(8)])),
        "dn": striped8(np.stack([np.random.permutation(S) for _ in range(8)])),
        "slot": striped8(np.stack([np.random.permutation(U)[:S] for _ in range(8)])),
    }


def reference(x_words, x_scales, w1, gn, w2, mem, offs, rt, lf, up, dn, slot):
    xq = unpack_weight(x_words, x_scales)[:, unstriped(offs)]
    y = mxq(f64(w1), 0, "e4m3").T @ xq
    dx = y[np.arange(H)[:, None], runs(rt, H)] - (y[np.arange(H)[:, None], runs(lf, H)])
    dy = y[np.arange(H)[:, None], runs(up, H)] - (y[np.arange(H)[:, None], runs(dn, H)])
    z = f64(gn) * (np.sqrt(0.25 * ((dx) ** 2 + (dy) ** 2) + 0.05))
    h = mxq(f64(w2), 0, "e4m3").T @ mxq(z, 0, "e4m3")
    out = f64(mem).copy()
    out[np.arange(N)[:, None], runs(slot, N)] = h
    return out

from contextlib import ExitStack

import concourse.mybir as mybir
from concourse.masks import make_identity

K, T, S, N, H, U = 512, 2048, 512, 512, 512, 1024
FLOPS = 2 * K * H * S + 2 * H * N * S

F32 = mybir.dt.float32
BF16 = mybir.dt.bfloat16
I32 = mybir.dt.int32
U32 = mybir.dt.uint32
U16 = mybir.dt.uint16
U8 = mybir.dt.uint8
FP8X4 = mybir.dt.float8_e4m3fn_x4
ACT = mybir.ActivationFunctionType
ALU = mybir.AluOpType

P = 128
PACK = 4
HALF = S // 2
COLS = HALF // 16
W1_SPLIT = 80


def tile_picked_gradmag_none_p_kernel(
    tc, x_words, x_scales, w1, gn, w2, mem, offs, rt, lf, up, dn, slot, out
):
    nc = tc.nc
    with ExitStack() as ctx:
        keep = ctx.enter_context(tc.tile_pool(name="keep", bufs=1))
        ring = ctx.enter_context(tc.tile_pool(name="ring", bufs=3))
        psum = ctx.enter_context(tc.psum_pool(name="psum", bufs=1))

        def load_list(source, name):
            tile = keep.tile([P, S // 16], U16, name=name)
            nc.sync.dma_start(tile[:], source)
            return tile

        offs_sb = load_list(offs, "offs_sb")
        w1_rows = w1.rearrange("(p j) c -> p j c", j=PACK)
        w1_lo = keep.tile([P, PACK, H // 2], F32, name="w1_lo")
        nc.sync.dma_start(w1_lo[:], w1_rows[:, :, : H // 2])
        xs_all = keep.tile([P, T], U8, name="xs_all")
        nc.vector.memset(xs_all[:].bitcast(I32), 0)
        xs_rows = x_scales[0].bitcast(I32)
        for r in range(4):
            nc.sync.dma_start(xs_all[:].bitcast(I32)[r:P:32, :], xs_rows[r:16:4, :])

        w1_hi = keep.tile([P, PACK, H // 2], F32, name="w1_hi")
        nc.sync.dma_start(w1_hi[:], w1_rows[:, :, H // 2 :])
        x_all = keep.tile([P, T], I32, name="x_all")
        nc.sync.dma_start(x_all[:], x_words[0].rearrange("p n r -> p (n r)").bitcast(I32))

        rt_sb = load_list(rt, "rt_sb")
        lf_sb = load_list(lf, "lf_sb")
        up_sb = load_list(up, "up_sb")
        dn_sb = load_list(dn, "dn_sb")
        gain = keep.tile([P, PACK], F32, name="gain")
        nc.sync.dma_start(gain[:], gn.rearrange("(p t) o -> p (t o)", t=PACK))
        w2_raw = keep.tile([P, PACK, N], F32, name="w2_raw")
        nc.sync.dma_start(w2_raw[:], w2.rearrange("(p j) c -> p j c", j=PACK))
        slot_sb = load_list(slot, "slot_sb")
        mem_rows = mem.rearrange("(p t) w -> t p w", t=PACK)
        out_rows = out.rearrange("(p t) w -> t p w", t=PACK)
        pages = []
        for t in range(PACK):
            page = keep.tile([P, U], F32, name="page%d" % t)
            nc.sync.dma_start(page[:], mem_rows[t])
            pages.append(page)

        ident = keep.tile([P, P], F32, name="ident")
        make_identity(nc, ident[:])
        warm = keep.tile([P, 1], F32, name="warm")
        nc.scalar.activation(warm[:], ident[:, 0:1], ACT.Sqrt)

        xs = keep.tile([P, S], U8, name="xs", align_bytes=64)
        nc.vector.tensor_copy(xs[:], xs_all[:].indirect(offs_sb[:]))

        def dealt_views(raw, grouped):
            return (
                grouped[:].rearrange("p (t m j) -> p m t j", t=PACK, j=PACK),
                raw[:].rearrange("p j (m t) -> p m t j", t=PACK),
            )

        w1_bf = keep.tile([P, PACK * H], BF16, name="w1_bf", align_bytes=64)
        dst, src = dealt_views(w1_lo, w1_bf)
        nc.scalar.copy(dst[:, :64], src)
        dst, src = dealt_views(w1_hi, w1_bf)
        nc.vector.tensor_copy(dst[:, 64:96], src[:, :32])
        nc.scalar.copy(dst[:, 96:], src[:, 32:])
        w1_q = keep.tile([P, H], U32, name="w1_q", tag="w1_q", align_bytes=64)
        w1_s = keep.tile([P, H], U8, name="w1_s", align_bytes=64)
        nc.vector.quantize_mx(out=w1_q[:].bitcast(FP8X4), scales=w1_s[:], in_=w1_bf[:])

        xq = keep.tile([P, S], U32, name="xq", align_bytes=64)
        for c in range(2):
            nc.vector.tensor_copy(
                xq[:, c * HALF : (c + 1) * HALF],
                x_all[:].bitcast(U32).indirect(offs_sb[:, c * COLS : (c + 1) * COLS]),
            )

        def product(acc, w_q, w_s, t, a_q, a_s):
            cols = slice(t * P, (t + 1) * P)
            nc.tensor.matmul_mx(
                out=acc,
                lhsT=w_q[:, cols].bitcast(FP8X4),
                lhsT_scale=w_s[:, cols],
                rhs=a_q.bitcast(FP8X4),
                rhs_scale=a_s,
                start=True,
                stop=True,
            )

        ys = []
        for t in range(PACK):
            y = keep.tile([P, S], F32, name="y%d" % t)
            pieces = [slice(0, HALF), slice(HALF, S)] if t == 0 else [slice(0, S)]
            for cols in pieces:
                acc = psum.tile([P, cols.stop - cols.start], F32, name="acc", tag="acc", bufs=4)
                product(acc[:], w1_q, w1_s, t, xq[:, cols], xs[:, cols])
                nc.scalar.copy(y[:, cols], acc[:])
            ys.append(y)

        w2_bf = keep.tile([P, PACK * N], BF16, name="w2_bf", tag="w1_q", align_bytes=64)
        w2_dst, w2_src = dealt_views(w2_raw, w2_bf)
        w2_q = keep.tile([P, N], U32, name="w2_q", align_bytes=64)
        w2_s = keep.tile([P, N], U8, name="w2_s", align_bytes=64)

        def fetch(c, t, first_tag=None):
            cols = slice(c * COLS, (c + 1) * COLS)
            got = []
            if first_tag:
                four = keep.tile([P, 4, HALF], F32, name="four", tag=first_tag, align_bytes=64)
            for n, lists in enumerate((rt_sb, lf_sb, up_sb, dn_sb)):
                if first_tag:
                    g = four[:, n, :]
                else:
                    g = keep.tile([P, HALF], F32, name="got", tag="got%d" % n, bufs=2)[:]
                window = ys[t][:].indirect(lists[:, cols])
                if n % 2 == 0:
                    nc.vector.tensor_copy(g, window)
                else:
                    nc.vector.tensor_scalar(g, window, -1.0, 0.0, ALU.mult, ALU.add)
                got.append(g)
            return got

        def add_turned(dst, a, b):
            nc.tensor.matmul(dst, a, ident[:], start=True, stop=False, is_transpose=True)
            nc.tensor.matmul(dst, b, ident[:], start=False, stop=True, is_transpose=True)

        def differences(got, tag="squares", bufs=3):
            diffs = psum.tile([P, 2, 2, P], F32, name="diffs", tag="diffs", bufs=2)
            for d in range(2):
                for b in range(2):
                    blk = slice(b * P, (b + 1) * P)
                    add_turned(diffs[:, d, b, :], got[2 * d][:, blk], got[2 * d + 1][:, blk])
            squares = keep.tile([P, 2, 2, P], F32, name="squares", tag=tag, bufs=bufs)
            nc.scalar.activation(squares[:], diffs[:], ACT.Square)
            return squares

        def magnitude(squares, t, z):
            total = psum.tile([P, 2, P], F32, name="total", tag="total", bufs=2)
            for b in range(2):
                add_turned(total[:, b, :], squares[:, 0, b, :], squares[:, 1, b, :])
            root = ring.tile([P, HALF], F32, name="root")
            nc.scalar.activation(
                root[:], total[:].rearrange("p b j -> p (b j)"), ACT.Sqrt, bias=0.05, scale=0.25
            )
            nc.scalar.activation(
                z[:].rearrange("p (j t) -> p j t", t=PACK)[:, :, t],
                root[:],
                ACT.Copy,
                scale=gain[:, t : t + 1],
            )

        def quantise(c, z):
            z_q = keep.tile([P, HALF], U32, name="z_q%d" % c, align_bytes=64)
            z_s = keep.tile([P, HALF], U8, name="z_s%d" % c, align_bytes=64)
            nc.vector.quantize_mx(out=z_q[:].bitcast(FP8X4), scales=z_s[:], in_=z[:])
            return z_q, z_s

        def second(t, parts, name):
            acc = psum.tile([P, len(parts) * HALF], F32, name="acc", tag="acc", bufs=4)
            for n, (z_q, z_s) in enumerate(parts):
                product(acc[:, n * HALF : (n + 1) * HALF], w2_q, w2_s, t, z_q[:], z_s[:])
            h = keep.tile([P, len(parts) * HALF], F32, name=name, tag=name)
            nc.scalar.copy(h[:], acc[:])
            return h

        def put(t, h, cols):
            nc.vector.tensor_copy(pages[t][:].indirect(slot_sb[:, cols]), h[:])

        first, second_cols = slice(0, COLS), slice(COLS, 2 * COLS)
        z0 = keep.tile([P, PACK * HALF], BF16, name="z0", tag="z0", align_bytes=64)
        z1 = keep.tile([P, PACK * HALF], BF16, name="z1", align_bytes=64)
        zs = (z0, z1)
        steps = [(c, t) for c in range(2) for t in range(PACK)]
        pending = None
        for n, (c, t) in enumerate(steps[:-1]):
            squares = differences(fetch(c, t))
            if pending:
                magnitude(*pending)
            pending = (squares, t, zs[c])
            if n < PACK:
                part = slice(32 * n, 32 * (n + 1))
                nc.scalar.copy(w2_dst[:, part], w2_src[:, part])
        nc.vector.quantize_mx(out=w2_q[:].bitcast(FP8X4), scales=w2_s[:], in_=w2_bf[:])
        zq0 = quantise(0, z0)
        got = fetch(1, PACK - 1, "z0")
        early = [second(t, [zq0], "h0%d" % t) for t in range(PACK - 1)]
        squares = differences(got, "h03", 1)
        magnitude(*pending)
        magnitude(squares, PACK - 1, z1)
        for t in range(PACK - 1):
            put(t, early[t], first)
        zq1 = quantise(1, z1)
        put(PACK - 1, second(PACK - 1, [zq0], "h03"), first)
        for t in range(PACK):
            put(t, second(t, [zq1], "h1%d" % t), second_cols)
            nc.sync.dma_start(out_rows[t], pages[t][:])
